import numpy as np
import ml_dtypes


def mxq(x, axis, fmt="e4m3"):
    dtype, down = {"e4m3": (ml_dtypes.float8_e4m3fn, 7), "e5m2": (ml_dtypes.float8_e5m2, 14)}[fmt]
    v = np.moveaxis(np.asarray(x, np.float32).astype(ml_dtypes.bfloat16).astype(np.float64), axis, -1)
    blocks = v.reshape(v.shape[:-1] + (-1, 32))
    amax = np.abs(blocks).max(-1, keepdims=True)
    byte = np.maximum(np.where(amax > 0, np.frexp(amax)[1] - 1 + 127, 0) - down, 1)
    scale = np.exp2(byte - 127.0)
    codes = (blocks / scale).astype(np.float32).astype(dtype).astype(np.float64)
    return np.moveaxis((codes * scale).reshape(v.shape), -1, axis)


WIDE = False


def mx_kscale(k):
    if not WIDE:
        return np.ones(k)
    levels = np.array([10, -10, 5, -5, 0])
    if k % 512:
        return np.exp2(np.random.permutation(np.resize(levels, k // 32))).repeat(32)
    a = np.empty((k // 512, 16))
    for p in range(k // 512):
        a[p, :8] = np.random.permutation(np.resize(levels, 8))
        for g in range(8):
            far = levels[np.abs(levels - a[p, g]) >= 10]
            a[p, g + 8] = far[np.random.randint(len(far))]
    return np.exp2(a.ravel()).repeat(32)


BF16 = ml_dtypes.bfloat16


def bf(x):
    return np.asarray(x, np.float32).astype(BF16)


def f64(x):
    return np.asarray(x).astype(np.float64)


T, D, DS, F = 128, 2048, 2048, 2048


def sigmoid(v):
    return 1.0 / (1.0 + np.exp(-v))


def draw0():
    s, r, t = mx_kscale(D), mx_kscale(DS), mx_kscale(F)
    return {
        "k_recv": bf(np.random.standard_normal((T, D)) * s),
        "k_share": bf(np.random.standard_normal((T, DS)) * r),
        "w_recv": bf(np.random.standard_normal((D, F)) / np.sqrt(D) / s[:, None]),
        "w_share": bf(np.random.standard_normal((DS, F)) / np.sqrt(DS) / r[:, None]),
        "g_hid": bf((1.0 + 0.1 * np.random.standard_normal(F)) * t),
        "w_delta": bf(np.random.standard_normal((F, D)) * 2.0 / np.sqrt(F) / t[:, None] * s),
        "w_gate": bf(np.random.standard_normal((F, D)) * 1.5 / np.sqrt(F) / t[:, None]),
    }


def core(k_recv, k_share, w_recv, w_share, g_hid, w_delta, w_gate):
    kr = f64(k_recv)
    u = (mxq(kr, 1, "e4m3") @ mxq(f64(w_recv), 0, "e4m3")) + (mxq(f64(k_share), 1, "e4m3") @ mxq(f64(w_share), 0, "e4m3"))
    h = u * sigmoid(u) * f64(g_hid)[None, :]
    hq = mxq(h, 1, "e4m3")
    delta = hq @ mxq(f64(w_delta), 0, "e4m3")
    gate = sigmoid(hq @ mxq(f64(w_gate), 0, "e4m3"))
    return kr + gate * delta


def e4m3fn_bytes(y):
    return np.clip(np.asarray(y, np.float64), -448.0, 448.0).astype(np.float32).astype(ml_dtypes.float8_e4m3fn).view(np.uint8)


def e4m3fn_values(b):
    return np.asarray(b, np.uint8).view(ml_dtypes.float8_e4m3fn).astype(np.float64)


def setup_inputs():
    d = draw0()
    x0 = np.asarray(d['w_share']).astype(np.float64)
    s = (np.max(np.abs(x0), axis=(1,), keepdims=True) / 448.0).astype(np.float32)
    out = {}
    for k, v in d.items():
        if k == 'w_share':
            out['w_share_bytes'] = e4m3fn_bytes(x0 / s.astype(np.float64))
            out['w_share_scale'] = s
        else:
            out[k] = v
    return out


def reference(k_recv, k_share, w_recv, w_share_bytes, w_share_scale, g_hid, w_delta, w_gate):
    return core(k_recv, k_share, w_recv, e4m3fn_values(w_share_bytes) * w_share_scale.astype(np.float64), g_hid, w_delta, w_gate)

@@ -1,0 +1,313 @@
+from contextlib import ExitStack
+
+import concourse.mybir as mybir
+from concourse.masks import make_identity
+
+F32 = mybir.dt.float32
+BF16 = mybir.dt.bfloat16
+U32 = mybir.dt.uint32
+U8 = mybir.dt.uint8
+FP8 = mybir.dt.float8_e4m3fn
+FP8X4 = mybir.dt.float8_e4m3fn_x4
+ACT = mybir.ActivationFunctionType
+MULT = mybir.AluOpType.mult
+ADD = mybir.AluOpType.add
+
+P = 128
+T = 128
+D = 2048
+PASSES = 4
+FLOPS = 4 * 2 * T * D * D
+
+SHARE_V_COLS = 896
+
+
+def tile_cachetocachegatedkeyfuser_w_kernel(
+    tc, k_recv, k_share, w_recv, w_share_bytes, w_share_scale, g_hid, w_delta, w_gate, out
+):
+    nc = tc.nc
+
+    chunks = []
+    for g in range(4):
+        for c in range(2):
+            chunks.append(("share", g, 1024 * c, 1024, None))
+    for g in range(4):
+        for c in range(2):
+            chunks.append(("recv", g, 1024 * c, 1024, g))
+    for g in range(4):
+        for c in range(2):
+            chunks.append(("gate", g, 1024 * c, 1024, 4 + g))
+    for c0, width in ((0, 1024), (1024, 512), (1536, 512)):
+        for g in range(4):
+            chunks.append(("delta", g, c0, width, 8 + g))
+    n_chunks = len(chunks)
+    raw_src = [w_recv, w_gate, w_delta]
+
+    with ExitStack() as ctx:
+        keep = ctx.enter_context(tc.tile_pool(name="keep", bufs=1))
+        raws = ctx.enter_context(tc.tile_pool(name="raws", bufs=5))
+        groups = ctx.enter_context(tc.tile_pool(name="groups", bufs=3))
+        quant = ctx.enter_context(tc.tile_pool(name="quant", bufs=8))
+        psum = ctx.enter_context(tc.psum_pool(name="psum", bufs=1))
+        ctx.enter_context(tc.manual_schedule())
+        pools = {}
+        early = {}
+
+        scale = keep.tile([P, PASSES, 4], F32, name="scale")
+        nc.scalar.dma_start(out=scale[:], in_=w_share_scale.rearrange("(g p t) o -> p g (t o)", p=P, t=4))
+        ident = keep.tile([P, P], F32, name="ident")
+        make_identity(nc, ident[:])
+        warm = keep.tile([P, 1], F32, name="warm")
+        nc.vector.memset(warm[:], 0.0)
+        nc.scalar.activation(out=warm[:], in_=warm[:], func=ACT.Silu)
+
+        bytes_view = w_share_bytes.rearrange("(g p t) n -> g p t n", p=P, t=4)
+        byte_tiles = []
+
+        def load_bytes(i):
+            t = pools["share"].tile([P, 4, 1024], U8, name="codes_in", tag="codes_in", bufs=8, align_bytes=64)
+            _, g, c0, width, _ = chunks[i]
+            nc.sync.dma_start(out=t[:], in_=bytes_view[g][:, :, c0 : c0 + width])
+            byte_tiles.append(t)
+
+        kr = keep.tile([T, D], BF16, name="kr", align_bytes=64)
+        gain = keep.tile([P, D], BF16, name="gain", align_bytes=64)
+        raw_tiles = []
+
+        def load_raw(i):
+            t = raws.tile([P, 4, D], BF16, name="raw", tag="raw", align_bytes=64)
+            view = raw_src[i // 4].rearrange("(g p t) n -> g p t n", p=P, t=4)
+            nc.sync.dma_start(out=t[:], in_=view[i % 4])
+            raw_tiles.append(t)
+
+        wide_tiles = {}
+        group_tiles = {}
+        code_tiles = {}
+
+        def widen(i):
+            g = chunks[i][1]
+            t = pools["share"].tile([P, 4, 1024], BF16, name="wide", tag="wide", bufs=3, align_bytes=64)
+            wide_tiles[i] = t
+            src = byte_tiles[i]
+            n_scalar = 1 if i == 0 else 3
+            for j in range(4):
+                col = scale[:, g, j : j + 1]
+                if j < n_scalar:
+                    nc.scalar.activation(out=t[:, j, :], in_=src[:, j, :].bitcast(FP8), func=ACT.Copy, scale=col)
+                else:
+                    nc.vector.tensor_scalar(
+                        out=t[:, j, :], in0=src[:, j, :].bitcast(FP8), scalar1=col, scalar2=None, op0=MULT
+                    )
+
+        def interleave(i):
+            name, g, c0, width, raw = chunks[i]
+            dst = groups.tile([P, 4 * width], BF16, name="group", tag="group", align_bytes=64)
+            group_tiles[i] = dst
+            if name == "share":
+                src = wide_tiles.pop(i)[:, :, 0:width]
+                cut = 640 if i == 0 else SHARE_V_COLS
+            else:
+                src = raw_tiles[raw][:, :, c0 : c0 + width]
+                cut = width // 2
+            for copy, lo, hi in ((nc.scalar.copy, cut, width), (nc.vector.tensor_copy, 0, cut)):
+                copy(
+                    out=dst[:, 4 * lo : 4 * hi].rearrange("p (c i t) -> p c t i", i=4, t=4),
+                    in_=src[:, :, lo:hi].rearrange("p t (c i) -> p c t i", i=4),
+                )
+
+        def quantize(i):
+            width = chunks[i][3]
+            codes = quant.tile([P, width], U32, name="wq", tag="wq", align_bytes=64)
+            scales = quant.tile([P, width], U8, name="ws", tag="ws", align_bytes=64)
+            nc.vector.quantize_mx(out=codes[:].bitcast(FP8X4), scales=scales[:], in_=group_tiles.pop(i)[:])
+            code_tiles[i] = (codes, scales)
+
+        def bank(b, shape, name):
+            return psum.tile(shape, F32, name=name, tag="bank%d" % b)
+
+        def transpose_half(x, half, b):
+            words = x[:].bitcast(F32)
+            xt = bank(b, [P, 4, T], "xt")
+            for gl in range(2):
+                g = 2 * half + gl
+                for u in range(2):
+                    nc.tensor.transpose(xt[:, 2 * gl + u, :], words[:, 256 * g + u : 256 * (g + 1) : 2], ident[:])
+            return xt
+
+        def regroup_half(copy, dst, xt, half):
+            copy(
+                out=dst[:].bitcast(F32)[:, 512 * half : 512 * (half + 1)].rearrange("p (g r u) -> p g r u", g=2, u=2),
+                in_=xt[:].rearrange("p (g u) r -> p g r u", g=2),
+            )
+
+        def new_operand(name):
+            grouped = keep.tile([P, 4 * 4 * T], BF16, name="xgroup", tag="xgroup", bufs=2, align_bytes=64)
+            codes = keep.tile([P, 4 * T], U32, name=name + "_q", align_bytes=64)
+            scales = keep.tile([P, 4 * T], U8, name=name + "_s", align_bytes=64)
+            return grouped, codes, scales
+
+        def quantize_operand(x, lo, hi):
+            grouped, codes, scales = x
+            nc.vector.quantize_mx(
+                out=codes[:, lo:hi].bitcast(FP8X4), scales=scales[:, lo:hi], in_=grouped[:, 4 * lo : 4 * hi]
+            )
+
+        acc = {}
+        operand = {}
+
+        def multiply(i):
+            name, g, c0, width, _ = chunks[i]
+            codes, scales = code_tiles.pop(i)
+            _, xq, xs = operand[name]
+            for n0 in range(0, width, 512):
+                b = (c0 + n0) // 512
+                first = name in ("share", "gate", "delta") and g == 0
+                last = name in ("recv", "gate", "delta") and g == 3
+                key = ("u" if name in ("share", "recv") else name, b)
+                if first:
+                    acc[key] = bank(b + (4 if name == "gate" else 0), [T, 512], "acc")
+                nc.tensor.matmul_mx(
+                    out=acc[key][:],
+                    lhsT=xq[:, g * T : (g + 1) * T].bitcast(FP8X4),
+                    lhsT_scale=xs[:, g * T : (g + 1) * T],
+                    rhs=codes[:, n0 : n0 + 512].bitcast(FP8X4),
+                    rhs_scale=scales[:, n0 : n0 + 512],
+                    start=first,
+                    stop=last,
+                )
+
+        late = {}
+
+        def silu(b):
+            t = pools["late"].tile([T, 512], F32, name="act", tag="act", bufs=4)
+            nc.scalar.activation(out=t[:], in_=acc[("u", b)][:], func=ACT.Silu)
+            late["act", b] = t
+
+        def gain_mul(b):
+            cols = slice(512 * b, 512 * (b + 1))
+            nc.vector.tensor_tensor(out=late["h"][:, cols], in0=late["act", b][:], in1=gain[:, cols], op=MULT)
+
+        def sigmoid(b):
+            cols = slice(512 * b, 512 * (b + 1))
+            nc.scalar.activation(out=late["gate"][:, cols], in_=acc[("gate", b)][:], func=ACT.Sigmoid)
+
+        def gated(b, lo=0, hi=512):
+            t = pools["late"].tile([T, hi - lo], F32, name="prod", tag="prod", bufs=3)
+            nc.vector.tensor_tensor(
+                out=t[:], in0=acc[("delta", b)][:, lo:hi], in1=late["gate"][:, 512 * b + lo : 512 * b + hi], op=MULT
+            )
+            late["prod", b, lo] = t
+
+        def residual(b, lo=0, hi=512):
+            cols = slice(512 * b + lo, 512 * b + hi)
+            t = pools["late"].tile([T, hi - lo], F32, name="res", tag="res", bufs=3)
+            nc.vector.tensor_tensor(out=t[:], in0=late["prod", b, lo][:], in1=kr[:, cols], op=ADD)
+            nc.sync.dma_start(out=out[:, cols], in_=t[:])
+
+        operand["share"] = new_operand("ks")
+        operand["recv"] = new_operand("kr")
+        xt = {}
+        gate_next = [16]
+
+        def step(s):
+            if 0 <= s + 1 < n_chunks:
+                interleave(s + 1)
+                name, g, c0, width, raw = chunks[s + 1]
+                if name in ("recv", "gate") and c0 == 1024 and raw + 5 < 12:
+                    load_raw(raw + 5)
+            if s + 2 < 8:
+                widen(s + 2)
+
+            if s == -1:
+                xt[0] = transpose_half(early["ks"], 0, 4)
+                xt[1] = transpose_half(early["ks"], 1, 5)
+            if s == 0:
+                regroup_half(nc.scalar.copy, operand["share"][0], xt[0], 0)
+                regroup_half(nc.scalar.copy, operand["share"][0], xt[1], 1)
+            if s == 3:
+                xt[0] = transpose_half(kr, 0, 6)
+                xt[1] = transpose_half(kr, 1, 7)
+            if s == 4:
+                regroup_half(nc.scalar.copy, operand["recv"][0], xt[0], 0)
+                regroup_half(nc.scalar.copy, operand["recv"][0], xt[1], 1)
+            if s == 1:
+                quantize_operand(operand["share"], 0, 512)
+            if s == 5:
+                quantize_operand(operand["recv"], 0, 512)
+            if s == 15:
+                silu(0)
+                silu(1)
+            if s == 16:
+                silu(2)
+                silu(3)
+                gain_mul(0)
+                gain_mul(1)
+                operand["gate"] = operand["delta"] = new_operand("hq")
+                xt[0] = transpose_half(late["h"], 0, 6)
+            if s == 17:
+                regroup_half(nc.scalar.copy, operand["gate"][0], xt[0], 0)
+                gain_mul(2)
+                gain_mul(3)
+                xt[1] = transpose_half(late["h"], 1, 7)
+            if s == 18:
+                quantize_operand(operand["gate"], 0, 256)
+                regroup_half(nc.scalar.copy, operand["gate"][0], xt[1], 1)
+            if s == 19:
+                quantize_operand(operand["gate"], 256, 512)
+            if s == 24:
+                sigmoid(0)
+                sigmoid(1)
+            if s == 25:
+                sigmoid(2)
+                sigmoid(3)
+            if s == 29:
+                gated(0)
+            if s == 30:
+                gated(1)
+                residual(0)
+            if s == 31:
+                residual(1)
+            if s == 33:
+                gated(2)
+            if s == 34:
+                residual(2)
+
+            if s >= 0:
+                quantize(s)
+                if s == 1:
+                    multiply(0)
+                if 1 <= s < 16:
+                    multiply(s)
+                elif s >= 18:
+                    stop = min(gate_next[0] + 2, s + 1)
+                    for i in range(gate_next[0], stop):
+                        multiply(i)
+                    gate_next[0] = stop
+
+        with tc.tile_pool(name="share", bufs=1) as share:
+            pools["share"] = share
+            early["ks"] = share.tile([T, D], BF16, name="ks", align_bytes=64)
+            load_bytes(0)
+            load_bytes(1)
+            nc.sync.dma_start(out=early["ks"][:], in_=k_share)
+            for i in range(2, 8):
+                load_bytes(i)
+            nc.sync.dma_start(out=kr[:], in_=k_recv)
+            load_raw(0)
+            load_raw(1)
+            nc.sync.dma_start(out=gain[:], in_=g_hid.partition_broadcast(P))
+            for i in range(2, 5):
+                load_raw(i)
+            for s in range(-2, 9):
+                step(s)
+
+        with tc.tile_pool(name="late", bufs=1) as late_pool:
+            pools["late"] = late_pool
+            late["h"] = late_pool.tile([T, D], BF16, name="h", align_bytes=64)
+            late["gate"] = late_pool.tile([T, D], F32, name="gate")
+            for s in range(9, n_chunks):
+                step(s)
+            gated(3, 0, 256)
+            gated(3, 256, 512)
+            residual(3, 0, 256)
+            residual(3, 256, 512)

@@ -19,7 +19,7 @@ D = 2048
 PASSES = 4
 FLOPS = 4 * 2 * T * D * D
 
-SHARE_V_COLS = 896
+SHARE_V_COLS = 928
 
 
 def tile_cachetocachegatedkeyfuser_w_kernel(
@@ -27,27 +27,53 @@ def tile_cachetocachegatedkeyfuser_w_kernel(
 ):
     nc = tc.nc
 
-    chunks = []
+    chunks = [("share", 0, 0, 512, None), ("share", 0, 512, 512, None), ("share", 0, 1024, 1024, None)]
+    for g in range(1, 4):
+        for c0 in (0, 1024):
+            chunks.append(("share", g, c0, 1024, None))
+    first_recv = len(chunks)
     for g in range(4):
-        for c in range(2):
-            chunks.append(("share", g, 1024 * c, 1024, None))
+        for c0 in (0, 1024):
+            chunks.append(("recv", g, c0, 1024, g))
+    first_gate = len(chunks)
     for g in range(4):
-        for c in range(2):
-            chunks.append(("recv", g, 1024 * c, 1024, g))
-    for g in range(4):
-        for c in range(2):
-            chunks.append(("gate", g, 1024 * c, 1024, 4 + g))
-    for c0, width in ((0, 1024), (1024, 512), (1536, 512)):
+        for c0 in (0, 1024):
+            chunks.append(("gate", g, c0, 1024, 4 + g))
+    first_delta = len(chunks)
+    for c0, width in ((0, 1024), (1024, 512), (1536, 256), (1792, 256)):
         for g in range(4):
             chunks.append(("delta", g, c0, width, 8 + g))
     n_chunks = len(chunks)
+    n_share, R, G, L = first_recv, first_recv, first_gate, first_delta
+
+    tensor_cols = {}
+    bank_of = {}
+    for k, i in enumerate(range(R, G)):
+        tensor_cols[i] = 256
+        bank_of[i] = 4 + k % 4
+    for k, i in enumerate(range(G + 4, G + 8)):
+        tensor_cols[i] = 256
+        bank_of[i] = k % 2
+
+    def vector_cols(i):
+        name, _, c0, width, _ = chunks[i]
+        if name == "share":
+            return width - 64 if width == 512 else SHARE_V_COLS
+        if i in tensor_cols:
+            return 416
+        if name == "delta" and c0 >= 1024:
+            return (3 * width // 8) // 16 * 16
+        if i in (L + 2, L + 3):
+            return 640
+        return 512
+
     raw_src = [w_recv, w_gate, w_delta]
 
     with ExitStack() as ctx:
         keep = ctx.enter_context(tc.tile_pool(name="keep", bufs=1))
         raws = ctx.enter_context(tc.tile_pool(name="raws", bufs=5))
-        groups = ctx.enter_context(tc.tile_pool(name="groups", bufs=3))
-        quant = ctx.enter_context(tc.tile_pool(name="quant", bufs=8))
+        groups = ctx.enter_context(tc.tile_pool(name="groups", bufs=4))
+        quant = ctx.enter_context(tc.tile_pool(name="quant", bufs=6))
         psum = ctx.enter_context(tc.psum_pool(name="psum", bufs=1))
         ctx.enter_context(tc.manual_schedule())
         pools = {}
@@ -57,6 +83,8 @@ def tile_cachetocachegatedkeyfuser_w_kernel(
         nc.scalar.dma_start(out=scale[:], in_=w_share_scale.rearrange("(g p t) o -> p g (t o)", p=P, t=4))
         ident = keep.tile([P, P], F32, name="ident")
         make_identity(nc, ident[:])
+        ident_bf = keep.tile([P, P], BF16, name="ident_bf", align_bytes=64)
+        make_identity(nc, ident_bf[:])
         warm = keep.tile([P, 1], F32, name="warm")
         nc.vector.memset(warm[:], 0.0)
         nc.scalar.activation(out=warm[:], in_=warm[:], func=ACT.Silu)
@@ -65,9 +93,9 @@ def tile_cachetocachegatedkeyfuser_w_kernel(
         byte_tiles = []
 
         def load_bytes(i):
-            t = pools["share"].tile([P, 4, 1024], U8, name="codes_in", tag="codes_in", bufs=8, align_bytes=64)
+            t = pools["share"].tile([P, 4, 1024], U8, name="codes_in", tag="codes_in", bufs=6, align_bytes=64)
             _, g, c0, width, _ = chunks[i]
-            nc.sync.dma_start(out=t[:], in_=bytes_view[g][:, :, c0 : c0 + width])
+            nc.sync.dma_start(out=t[:, :, 0:width], in_=bytes_view[g][:, :, c0 : c0 + width])
             byte_tiles.append(t)
 
         kr = keep.tile([T, D], BF16, name="kr", align_bytes=64)
@@ -85,31 +113,52 @@ def tile_cachetocachegatedkeyfuser_w_kernel(
         code_tiles = {}
 
         def widen(i):
-            g = chunks[i][1]
-            t = pools["share"].tile([P, 4, 1024], BF16, name="wide", tag="wide", bufs=3, align_bytes=64)
+            _, g, _, width, _ = chunks[i]
+            t = pools["share"].tile([P, 4, 1024], BF16, name="wide", tag="wide", bufs=4, align_bytes=64)
             wide_tiles[i] = t
             src = byte_tiles[i]
-            n_scalar = 1 if i == 0 else 3
+            n_scalar = 2 if i == 0 else 3
             for j in range(4):
                 col = scale[:, g, j : j + 1]
+                dst = t[:, j, 0:width]
+                codes = src[:, j, 0:width].bitcast(FP8)
                 if j < n_scalar:
-                    nc.scalar.activation(out=t[:, j, :], in_=src[:, j, :].bitcast(FP8), func=ACT.Copy, scale=col)
+                    nc.scalar.activation(out=dst, in_=codes, func=ACT.Copy, scale=col)
                 else:
-                    nc.vector.tensor_scalar(
-                        out=t[:, j, :], in0=src[:, j, :].bitcast(FP8), scalar1=col, scalar2=None, op0=MULT
-                    )
+                    nc.vector.tensor_scalar(out=dst, in0=codes, scalar1=col, scalar2=None, op0=MULT)
+
+        def source(i):
+            name, _, c0, width, raw = chunks[i]
+            if name == "share":
+                return wide_tiles[i][:, :, 0:width]
+            return raw_tiles[raw][:, :, c0 : c0 + width]
+
+        tensor_tiles = {}
+
+        def tensor_interleave(i):
+            width = chunks[i][3]
+            pt = psum.tile([P, 1024], BF16, name="pt", tag="bank%d" % bank_of[i])
+            for m in range(2):
+                c = width - 256 + 128 * m
+                nc.tensor.matmul(
+                    pt[:, 512 * m : 512 * (m + 1)],
+                    lhsT=ident_bf[:],
+                    rhs=source(i)[:, :, c : c + 128].rearrange("p t n -> p n t"),
+                    start=True,
+                    stop=True,
+                )
+            tensor_tiles[i] = pt
 
         def interleave(i):
-            name, g, c0, width, raw = chunks[i]
+            width = chunks[i][3]
+            src = source(i)
             dst = groups.tile([P, 4 * width], BF16, name="group", tag="group", align_bytes=64)
             group_tiles[i] = dst
-            if name == "share":
-                src = wide_tiles.pop(i)[:, :, 0:width]
-                cut = 640 if i == 0 else SHARE_V_COLS
-            else:
-                src = raw_tiles[raw][:, :, c0 : c0 + width]
-                cut = width // 2
-            for copy, lo, hi in ((nc.scalar.copy, cut, width), (nc.vector.tensor_copy, 0, cut)):
+            v_end = vector_cols(i)
+            s_end = width - tensor_cols.get(i, 0)
+            if s_end < width:
+                nc.scalar.copy(out=dst[:, 4 * s_end : 4 * width], in_=tensor_tiles.pop(i)[:])
+            for copy, lo, hi in ((nc.scalar.copy, v_end, s_end), (nc.vector.tensor_copy, 0, v_end)):
                 copy(
                     out=dst[:, 4 * lo : 4 * hi].rearrange("p (c i t) -> p c t i", i=4, t=4),
                     in_=src[:, :, lo:hi].rearrange("p t (c i) -> p c t i", i=4),
@@ -155,68 +204,79 @@ def tile_cachetocachegatedkeyfuser_w_kernel(
         acc = {}
         operand = {}
 
+        delta_bank = {0: 0, 512: 1, 1024: 2, 1536: 3, 1792: 4}
+
         def multiply(i):
             name, g, c0, width, _ = chunks[i]
             codes, scales = code_tiles.pop(i)
             _, xq, xs = operand[name]
-            for n0 in range(0, width, 512):
-                b = (c0 + n0) // 512
+            n = min(width, 512)
+            for n0 in range(0, width, n):
+                col = c0 + n0
                 first = name in ("share", "gate", "delta") and g == 0
                 last = name in ("recv", "gate", "delta") and g == 3
-                key = ("u" if name in ("share", "recv") else name, b)
+                key = ("u" if name in ("share", "recv") else name, col)
                 if first:
-                    acc[key] = bank(b + (4 if name == "gate" else 0), [T, 512], "acc")
+                    b = delta_bank[col] if name == "delta" else col // 512 + (4 if name == "gate" else 0)
+                    acc[key] = bank(b, [T, 512], "acc")
                 nc.tensor.matmul_mx(
-                    out=acc[key][:],
+                    out=acc[key][:, 0:n],
                     lhsT=xq[:, g * T : (g + 1) * T].bitcast(FP8X4),
                     lhsT_scale=xs[:, g * T : (g + 1) * T],
-                    rhs=codes[:, n0 : n0 + 512].bitcast(FP8X4),
-                    rhs_scale=scales[:, n0 : n0 + 512],
+                    rhs=codes[:, n0 : n0 + n].bitcast(FP8X4),
+                    rhs_scale=scales[:, n0 : n0 + n],
                     start=first,
                     stop=last,
                 )
 
         late = {}
 
-        def silu(b):
+        def silu(col):
             t = pools["late"].tile([T, 512], F32, name="act", tag="act", bufs=4)
-            nc.scalar.activation(out=t[:], in_=acc[("u", b)][:], func=ACT.Silu)
-            late["act", b] = t
+            nc.scalar.activation(out=t[:], in_=acc[("u", col)][:], func=ACT.Silu)
+            late["act", col] = t
 
-        def gain_mul(b):
-            cols = slice(512 * b, 512 * (b + 1))
-            nc.vector.tensor_tensor(out=late["h"][:, cols], in0=late["act", b][:], in1=gain[:, cols], op=MULT)
+        def gain_mul(col):
+            cols = slice(col, col + 512)
+            nc.vector.tensor_tensor(out=late["h"][:, cols], in0=late["act", col][:], in1=gain[:, cols], op=MULT)
 
-        def sigmoid(b):
-            cols = slice(512 * b, 512 * (b + 1))
-            nc.scalar.activation(out=late["gate"][:, cols], in_=acc[("gate", b)][:], func=ACT.Sigmoid)
+        def sigmoid(col):
+            nc.scalar.activation(out=late["gate"][:, col : col + 512], in_=acc[("gate", col)][:], func=ACT.Sigmoid)
 
-        def gated(b, lo=0, hi=512):
-            t = pools["late"].tile([T, hi - lo], F32, name="prod", tag="prod", bufs=3)
+        def gated(col, width=512):
+            t = pools["late"].tile([T, width], F32, name="prod", tag="prod", bufs=3)
             nc.vector.tensor_tensor(
-                out=t[:], in0=acc[("delta", b)][:, lo:hi], in1=late["gate"][:, 512 * b + lo : 512 * b + hi], op=MULT
+                out=t[:], in0=acc[("delta", col)][:, 0:width], in1=late["gate"][:, col : col + width], op=MULT
             )
-            late["prod", b, lo] = t
+            late["prod", col] = t
 
-        def residual(b, lo=0, hi=512):
-            cols = slice(512 * b + lo, 512 * b + hi)
-            t = pools["late"].tile([T, hi - lo], F32, name="res", tag="res", bufs=3)
-            nc.vector.tensor_tensor(out=t[:], in0=late["prod", b, lo][:], in1=kr[:, cols], op=ADD)
+        def residual(col, width=512):
+            cols = slice(col, col + width)
+            t = pools["late"].tile([T, width], F32, name="res", tag="res", bufs=3)
+            nc.vector.tensor_tensor(out=t[:], in0=late["prod", col][:], in1=kr[:, cols], op=ADD)
             nc.sync.dma_start(out=out[:, cols], in_=t[:])
 
         operand["share"] = new_operand("ks")
         operand["recv"] = new_operand("kr")
         xt = {}
-        gate_next = [16]
+        gate_next = [G]
 
         def step(s):
-            if 0 <= s + 1 < n_chunks:
-                interleave(s + 1)
-                name, g, c0, width, raw = chunks[s + 1]
+            i = s + 2
+            if 0 <= i < n_chunks:
+                interleave(i)
+                name, g, c0, width, raw = chunks[i]
                 if name in ("recv", "gate") and c0 == 1024 and raw + 5 < 12:
                     load_raw(raw + 5)
-            if s + 2 < 8:
-                widen(s + 2)
+            if s + 4 < n_share:
+                widen(s + 4)
+                if len(byte_tiles) < n_share:
+                    load_bytes(len(byte_tiles))
+                    if len(byte_tiles) == n_share:
+                        for k in range(2, 5):
+                            load_raw(k)
+            if s + 3 in tensor_cols:
+                tensor_interleave(s + 3)
 
             if s == -1:
                 xt[0] = transpose_half(early["ks"], 0, 4)
@@ -224,64 +284,68 @@ def tile_cachetocachegatedkeyfuser_w_kernel(
             if s == 0:
                 regroup_half(nc.scalar.copy, operand["share"][0], xt[0], 0)
                 regroup_half(nc.scalar.copy, operand["share"][0], xt[1], 1)
+            if s == 1:
+                quantize_operand(operand["share"], 0, 512)
             if s == 3:
                 xt[0] = transpose_half(kr, 0, 6)
                 xt[1] = transpose_half(kr, 1, 7)
             if s == 4:
                 regroup_half(nc.scalar.copy, operand["recv"][0], xt[0], 0)
                 regroup_half(nc.scalar.copy, operand["recv"][0], xt[1], 1)
-            if s == 1:
-                quantize_operand(operand["share"], 0, 512)
             if s == 5:
                 quantize_operand(operand["recv"], 0, 512)
-            if s == 15:
+            if s == G - 1:
                 silu(0)
-                silu(1)
-            if s == 16:
-                silu(2)
-                silu(3)
+                silu(512)
+            if s == G:
+                silu(1024)
+                silu(1536)
                 gain_mul(0)
-                gain_mul(1)
+                gain_mul(512)
                 operand["gate"] = operand["delta"] = new_operand("hq")
                 xt[0] = transpose_half(late["h"], 0, 6)
-            if s == 17:
+            if s == G + 1:
                 regroup_half(nc.scalar.copy, operand["gate"][0], xt[0], 0)
-                gain_mul(2)
-                gain_mul(3)
+                gain_mul(1024)
+                gain_mul(1536)
                 xt[1] = transpose_half(late["h"], 1, 7)
-            if s == 18:
+            if s == G + 2:
                 quantize_operand(operand["gate"], 0, 256)
                 regroup_half(nc.scalar.copy, operand["gate"][0], xt[1], 1)
-            if s == 19:
+            if s == G + 3:
                 quantize_operand(operand["gate"], 256, 512)
-            if s == 24:
+            if s == L:
                 sigmoid(0)
-                sigmoid(1)
-            if s == 25:
-                sigmoid(2)
-                sigmoid(3)
-            if s == 29:
+                sigmoid(512)
+            if s == L + 1:
+                sigmoid(1024)
+                sigmoid(1536)
+            if s == L + 5:
                 gated(0)
-            if s == 30:
-                gated(1)
+            if s == L + 6:
+                gated(512)
                 residual(0)
-            if s == 31:
-                residual(1)
-            if s == 33:
-                gated(2)
-            if s == 34:
-                residual(2)
+            if s == L + 7:
+                residual(512)
+            if s == L + 9:
+                gated(1024)
+            if s == L + 10:
+                residual(1024)
+            if s == L + 13:
+                gated(1536, 256)
+            if s == L + 14:
+                residual(1536, 256)
 
             if s >= 0:
                 quantize(s)
                 if s == 1:
                     multiply(0)
-                if 1 <= s < 16:
+                if 1 <= s < G:
                     multiply(s)
-                elif s >= 18:
+                elif s >= G + 2:
                     stop = min(gate_next[0] + 2, s + 1)
-                    for i in range(gate_next[0], stop):
-                        multiply(i)
+                    for k in range(gate_next[0], stop):
+                        multiply(k)
                     gate_next[0] = stop
 
         with tc.tile_pool(name="share", bufs=1) as share:
@@ -290,24 +354,20 @@ def tile_cachetocachegatedkeyfuser_w_kernel(
             load_bytes(0)
             load_bytes(1)
             nc.sync.dma_start(out=early["ks"][:], in_=k_share)
-            for i in range(2, 8):
+            for i in range(2, 6):
                 load_bytes(i)
             nc.sync.dma_start(out=kr[:], in_=k_recv)
             load_raw(0)
             load_raw(1)
             nc.sync.dma_start(out=gain[:], in_=g_hid.partition_broadcast(P))
-            for i in range(2, 5):
-                load_raw(i)
-            for s in range(-2, 9):
+            for s in range(-4, n_share):
                 step(s)
 
         with tc.tile_pool(name="late", bufs=1) as late_pool:
             pools["late"] = late_pool
             late["h"] = late_pool.tile([T, D], BF16, name="h", align_bytes=64)
             late["gate"] = late_pool.tile([T, D], F32, name="gate")
-            for s in range(9, n_chunks):
+            for s in range(n_share, n_chunks):
                 step(s)
-            gated(3, 0, 256)
-            gated(3, 256, 512)
-            residual(3, 0, 256)
-            residual(3, 256, 512)
+            gated(1792, 256)
+            residual(1792, 256)

@@ -19,7 +19,10 @@ D = 2048
 PASSES = 4
 FLOPS = 4 * 2 * T * D * D
 
-SHARE_V_COLS = 928
+PARAMS = dict(
+    ws=[512, 896] + [2560] * 3 + [3072] * 4,
+    vc=[448, 448] + [928] * 7 + [416] * 8 + [544] * 4 + [416] * 4 + [544] * 4 + [160] * 4 + [96] * 8,
+)
 
 
 def tile_cachetocachegatedkeyfuser_w_kernel(
@@ -56,16 +59,7 @@ def tile_cachetocachegatedkeyfuser_w_kernel(
         bank_of[i] = k % 2
 
     def vector_cols(i):
-        name, _, c0, width, _ = chunks[i]
-        if name == "share":
-            return width - 64 if width == 512 else SHARE_V_COLS
-        if i in tensor_cols:
-            return 416
-        if name == "delta" and c0 >= 1024:
-            return (3 * width // 8) // 16 * 16
-        if i in (L + 2, L + 3):
-            return 640
-        return 512
+        return PARAMS["vc"][i]
 
     raw_src = [w_recv, w_gate, w_delta]
 
@@ -93,9 +87,11 @@ def tile_cachetocachegatedkeyfuser_w_kernel(
         byte_tiles = []
 
         def load_bytes(i):
-            t = pools["share"].tile([P, 4, 1024], U8, name="codes_in", tag="codes_in", bufs=6, align_bytes=64)
             _, g, c0, width, _ = chunks[i]
-            nc.sync.dma_start(out=t[:, :, 0:width], in_=bytes_view[g][:, :, c0 : c0 + width])
+            t = pools["share"].tile(
+                [P, 4, width], U8, name="codes_in", tag="codes_in%d" % width, bufs={512: 2, 1024: 7}[width], align_bytes=64
+            )
+            nc.sync.dma_start(out=t[:], in_=bytes_view[g][:, :, c0 : c0 + width])
             byte_tiles.append(t)
 
         kr = keep.tile([T, D], BF16, name="kr", align_bytes=64)
@@ -114,18 +110,18 @@ def tile_cachetocachegatedkeyfuser_w_kernel(
 
         def widen(i):
             _, g, _, width, _ = chunks[i]
-            t = pools["share"].tile([P, 4, 1024], BF16, name="wide", tag="wide", bufs=4, align_bytes=64)
+            t = pools["share"].tile([P, 4, 1024], BF16, name="wide", tag="wide", bufs=3, align_bytes=64)
             wide_tiles[i] = t
             src = byte_tiles[i]
-            n_scalar = 2 if i == 0 else 3
             for j in range(4):
                 col = scale[:, g, j : j + 1]
-                dst = t[:, j, 0:width]
-                codes = src[:, j, 0:width].bitcast(FP8)
-                if j < n_scalar:
-                    nc.scalar.activation(out=dst, in_=codes, func=ACT.Copy, scale=col)
-                else:
-                    nc.vector.tensor_scalar(out=dst, in0=codes, scalar1=col, scalar2=None, op0=MULT)
+                cut = max(0, min(width, PARAMS["ws"][i] - j * width))
+                if cut:
+                    nc.scalar.activation(out=t[:, j, 0:cut], in_=src[:, j, 0:cut].bitcast(FP8), func=ACT.Copy, scale=col)
+                if cut < width:
+                    nc.vector.tensor_scalar(
+                        out=t[:, j, cut:width], in0=src[:, j, cut:width].bitcast(FP8), scalar1=col, scalar2=None, op0=MULT
+                    )
 
         def source(i):
             name, _, c0, width, raw = chunks[i]
@@ -134,6 +130,7 @@ def tile_cachetocachegatedkeyfuser_w_kernel(
             return raw_tiles[raw][:, :, c0 : c0 + width]
 
         tensor_tiles = {}
+        tensor_done = set()
 
         def tensor_interleave(i):
             width = chunks[i][3]
@@ -159,6 +156,8 @@ def tile_cachetocachegatedkeyfuser_w_kernel(
             if s_end < width:
                 nc.scalar.copy(out=dst[:, 4 * s_end : 4 * width], in_=tensor_tiles.pop(i)[:])
             for copy, lo, hi in ((nc.scalar.copy, v_end, s_end), (nc.vector.tensor_copy, 0, v_end)):
+                if lo == hi:
+                    continue
                 copy(
                     out=dst[:, 4 * lo : 4 * hi].rearrange("p (c i t) -> p c t i", i=4, t=4),
                     in_=src[:, :, lo:hi].rearrange("p t (c i) -> p c t i", i=4),
@@ -190,7 +189,7 @@ def tile_cachetocachegatedkeyfuser_w_kernel(
             )
 
         def new_operand(name):
-            grouped = keep.tile([P, 4 * 4 * T], BF16, name="xgroup", tag="xgroup", bufs=2, align_bytes=64)
+            grouped = keep.tile([P, 4 * 4 * T], BF16, name="xgroup", tag="xgroup", bufs=1, align_bytes=64)
             codes = keep.tile([P, 4 * T], U32, name=name + "_q", align_bytes=64)
             scales = keep.tile([P, 4 * T], U8, name=name + "_s", align_bytes=64)
             return grouped, codes, scales
@@ -270,13 +269,10 @@ def tile_cachetocachegatedkeyfuser_w_kernel(
                     load_raw(raw + 5)
             if s + 4 < n_share:
                 widen(s + 4)
-                if len(byte_tiles) < n_share:
-                    load_bytes(len(byte_tiles))
-                    if len(byte_tiles) == n_share:
-                        for k in range(2, 5):
-                            load_raw(k)
-            if s + 3 in tensor_cols:
-                tensor_interleave(s + 3)
+            for i in (s + 5 if s + 5 < G else s + 4, s + 4):
+                if i in tensor_cols and i not in tensor_done:
+                    tensor_done.add(i)
+                    tensor_interleave(i)
 
             if s == -1:
                 xt[0] = transpose_half(early["ks"], 0, 4)
@@ -284,7 +280,7 @@ def tile_cachetocachegatedkeyfuser_w_kernel(
             if s == 0:
                 regroup_half(nc.scalar.copy, operand["share"][0], xt[0], 0)
                 regroup_half(nc.scalar.copy, operand["share"][0], xt[1], 1)
-            if s == 1:
+            if s == 2:
                 quantize_operand(operand["share"], 0, 512)
             if s == 3:
                 xt[0] = transpose_half(kr, 0, 6)
@@ -292,7 +288,7 @@ def tile_cachetocachegatedkeyfuser_w_kernel(
             if s == 4:
                 regroup_half(nc.scalar.copy, operand["recv"][0], xt[0], 0)
                 regroup_half(nc.scalar.copy, operand["recv"][0], xt[1], 1)
-            if s == 5:
+            if s == 7:
                 quantize_operand(operand["recv"], 0, 512)
             if s == G - 1:
                 silu(0)
@@ -338,9 +334,10 @@ def tile_cachetocachegatedkeyfuser_w_kernel(
 
             if s >= 0:
                 quantize(s)
-                if s == 1:
+                if s == 2:
                     multiply(0)
-                if 1 <= s < G:
+                    multiply(1)
+                if 2 <= s < G:
                     multiply(s)
                 elif s >= G + 2:
                     stop = min(gate_next[0] + 2, s + 1)
@@ -351,15 +348,17 @@ def tile_cachetocachegatedkeyfuser_w_kernel(
         with tc.tile_pool(name="share", bufs=1) as share:
             pools["share"] = share
             early["ks"] = share.tile([T, D], BF16, name="ks", align_bytes=64)
-            load_bytes(0)
-            load_bytes(1)
+            for i in range(3):
+                load_bytes(i)
             nc.sync.dma_start(out=early["ks"][:], in_=k_share)
-            for i in range(2, 6):
+            for i in range(3, n_share):
                 load_bytes(i)
             nc.sync.dma_start(out=kr[:], in_=k_recv)
             load_raw(0)
             load_raw(1)
             nc.sync.dma_start(out=gain[:], in_=g_hid.partition_broadcast(P))
+            for i in range(2, 5):
+                load_raw(i)
             for s in range(-4, n_share):
                 step(s)
 

@@ -20,8 +20,9 @@ PASSES = 4
 FLOPS = 4 * 2 * T * D * D
 
 PARAMS = dict(
-    ws=[512, 896] + [2560] * 3 + [3072] * 4,
-    vc=[448, 448] + [928] * 7 + [416] * 8 + [544] * 4 + [416] * 4 + [544] * 4 + [160] * 4 + [96] * 8,
+    ws=[512, 640] + [2624] * 3 + [3072] * 4,
+    tail=((0, 1024), (1024, 512), (1536, 256), (1792, 256)),
+    vc=[480, 480] + [928] * 3 + [960] * 4 + [224] * 4 + [480] * 4 + [576] * 4 + [384] * 4 + [672] * 2 + [608] * 2 + [128] * 4 + [64] * 8,
 )
 
 
@@ -43,7 +44,7 @@ def tile_cachetocachegatedkeyfuser_w_kernel(
         for c0 in (0, 1024):
             chunks.append(("gate", g, c0, 1024, 4 + g))
     first_delta = len(chunks)
-    for c0, width in ((0, 1024), (1024, 512), (1536, 256), (1792, 256)):
+    for c0, width in PARAMS["tail"]:
         for g in range(4):
             chunks.append(("delta", g, c0, width, 8 + g))
     n_chunks = len(chunks)
@@ -203,7 +204,7 @@ def tile_cachetocachegatedkeyfuser_w_kernel(
         acc = {}
         operand = {}
 
-        delta_bank = {0: 0, 512: 1, 1024: 2, 1536: 3, 1792: 4}
+        delta_bank = {0: 0, 512: 1, 1024: 2, 1536: 3, 1792: 4, 1920: 5}
 
         def multiply(i):
             name, g, c0, width, _ = chunks[i]
@@ -239,26 +240,43 @@ def tile_cachetocachegatedkeyfuser_w_kernel(
             cols = slice(col, col + 512)
             nc.vector.tensor_tensor(out=late["h"][:, cols], in0=late["act", col][:], in1=gain[:, cols], op=MULT)
 
-        def sigmoid(col):
-            nc.scalar.activation(out=late["gate"][:, col : col + 512], in_=acc[("gate", col)][:], func=ACT.Sigmoid)
+        def half_tanh(col):
+            nc.scalar.activation(out=late["gate"][:, col : col + 512], in_=acc[("gate", col)][:], func=ACT.Tanh, scale=0.5)
 
         def gated(col, width=512):
             t = pools["late"].tile([T, width], F32, name="prod", tag="prod", bufs=3)
-            nc.vector.tensor_tensor(
-                out=t[:], in0=acc[("delta", col)][:, 0:width], in1=late["gate"][:, col : col + width], op=MULT
+            nc.vector.scalar_tensor_tensor(
+                out=t[:],
+                in0=late["gate"][:, col : col + width],
+                scalar=1.0,
+                in1=acc[("delta", col)][:, 0:width],
+                op0=ADD,
+                op1=MULT,
             )
             late["prod", col] = t
 
         def residual(col, width=512):
             cols = slice(col, col + width)
             t = pools["late"].tile([T, width], F32, name="res", tag="res", bufs=3)
-            nc.vector.tensor_tensor(out=t[:], in0=late["prod", col][:], in1=kr[:, cols], op=ADD)
+            nc.vector.scalar_tensor_tensor(
+                out=t[:], in0=late["prod", col][:], scalar=0.5, in1=kr[:, cols], op0=MULT, op1=ADD
+            )
             nc.sync.dma_start(out=out[:, cols], in_=t[:])
 
         operand["share"] = new_operand("ks")
         operand["recv"] = new_operand("kr")
         xt = {}
         gate_next = [G]
+
+        tail_calls = {}
+        done = L
+        for c0, width in PARAMS["tail"]:
+            done += 4
+            for k, col in enumerate(range(c0, c0 + width, 512)):
+                args = (col, min(width, 512))
+                last = (c0 + width) == D
+                tail_calls.setdefault(10**6 if last else done + 1 + k, []).append((args, gated))
+                tail_calls.setdefault(10**6 if last else done + 2 + k, []).append((args, residual))
 
         def step(s):
             i = s + 2
@@ -311,26 +329,13 @@ def tile_cachetocachegatedkeyfuser_w_kernel(
             if s == G + 3:
                 quantize_operand(operand["gate"], 256, 512)
             if s == L:
-                sigmoid(0)
-                sigmoid(512)
+                half_tanh(0)
+                half_tanh(512)
             if s == L + 1:
-                sigmoid(1024)
-                sigmoid(1536)
-            if s == L + 5:
-                gated(0)
-            if s == L + 6:
-                gated(512)
-                residual(0)
-            if s == L + 7:
-                residual(512)
-            if s == L + 9:
-                gated(1024)
-            if s == L + 10:
-                residual(1024)
-            if s == L + 13:
-                gated(1536, 256)
-            if s == L + 14:
-                residual(1536, 256)
+                half_tanh(1024)
+                half_tanh(1536)
+            for when, call in tail_calls.get(s, []):
+                call(*when)
 
             if s >= 0:
                 quantize(s)
@@ -368,5 +373,5 @@ def tile_cachetocachegatedkeyfuser_w_kernel(
             late["gate"] = late_pool.tile([T, D], F32, name="gate")
             for s in range(n_share, n_chunks):
                 step(s)
-            gated(1792, 256)
-            residual(1792, 256)
+            for when, call in tail_calls[10**6]:
+                call(*when)

from contextlib import ExitStack

import concourse.mybir as mybir
from concourse.masks import make_identity

F32 = mybir.dt.float32
BF16 = mybir.dt.bfloat16
U32 = mybir.dt.uint32
U8 = mybir.dt.uint8
FP8 = mybir.dt.float8_e4m3fn
FP8X4 = mybir.dt.float8_e4m3fn_x4
ACT = mybir.ActivationFunctionType
MULT = mybir.AluOpType.mult
ADD = mybir.AluOpType.add

P = 128
T = 128
D = 2048
PASSES = 4
FLOPS = 4 * 2 * T * D * D

PARAMS = dict(
    ws=[512, 640] + [2624] * 3 + [3072] * 4,
    tail=((0, 1024), (1024, 512), (1536, 256), (1792, 256)),
    vc=[480, 480] + [928] * 3 + [960] * 4 + [224] * 4 + [480] * 4 + [576] * 4 + [384] * 4 + [672] * 2 + [608] * 2 + [128] * 4 + [64] * 8,
)


def tile_cachetocachegatedkeyfuser_w_kernel(
    tc, k_recv, k_share, w_recv, w_share_bytes, w_share_scale, g_hid, w_delta, w_gate, out
):
    nc = tc.nc

    chunks = [("share", 0, 0, 512, None), ("share", 0, 512, 512, None), ("share", 0, 1024, 1024, None)]
    for g in range(1, 4):
        for c0 in (0, 1024):
            chunks.append(("share", g, c0, 1024, None))
    first_recv = len(chunks)
    for g in range(4):
        for c0 in (0, 1024):
            chunks.append(("recv", g, c0, 1024, g))
    first_gate = len(chunks)
    for g in range(4):
        for c0 in (0, 1024):
            chunks.append(("gate", g, c0, 1024, 4 + g))
    first_delta = len(chunks)
    for c0, width in PARAMS["tail"]:
        for g in range(4):
            chunks.append(("delta", g, c0, width, 8 + g))
    n_chunks = len(chunks)
    n_share, R, G, L = first_recv, first_recv, first_gate, first_delta

    tensor_cols = {}
    bank_of = {}
    for k, i in enumerate(range(R, G)):
        tensor_cols[i] = 256
        bank_of[i] = 4 + k % 4
    for k, i in enumerate(range(G + 4, G + 8)):
        tensor_cols[i] = 256
        bank_of[i] = k % 2

    def vector_cols(i):
        return PARAMS["vc"][i]

    raw_src = [w_recv, w_gate, w_delta]

    with ExitStack() as ctx:
        keep = ctx.enter_context(tc.tile_pool(name="keep", bufs=1))
        raws = ctx.enter_context(tc.tile_pool(name="raws", bufs=5))
        groups = ctx.enter_context(tc.tile_pool(name="groups", bufs=4))
        quant = ctx.enter_context(tc.tile_pool(name="quant", bufs=6))
        psum = ctx.enter_context(tc.psum_pool(name="psum", bufs=1))
        ctx.enter_context(tc.manual_schedule())
        pools = {}
        early = {}

        scale = keep.tile([P, PASSES, 4], F32, name="scale")
        nc.scalar.dma_start(out=scale[:], in_=w_share_scale.rearrange("(g p t) o -> p g (t o)", p=P, t=4))
        ident = keep.tile([P, P], F32, name="ident")
        make_identity(nc, ident[:])
        ident_bf = keep.tile([P, P], BF16, name="ident_bf", align_bytes=64)
        make_identity(nc, ident_bf[:])
        warm = keep.tile([P, 1], F32, name="warm")
        nc.vector.memset(warm[:], 0.0)
        nc.scalar.activation(out=warm[:], in_=warm[:], func=ACT.Silu)

        bytes_view = w_share_bytes.rearrange("(g p t) n -> g p t n", p=P, t=4)
        byte_tiles = []

        def load_bytes(i):
            _, g, c0, width, _ = chunks[i]
            t = pools["share"].tile(
                [P, 4, width], U8, name="codes_in", tag="codes_in%d" % width, bufs={512: 2, 1024: 7}[width], align_bytes=64
            )
            nc.sync.dma_start(out=t[:], in_=bytes_view[g][:, :, c0 : c0 + width])
            byte_tiles.append(t)

        kr = keep.tile([T, D], BF16, name="kr", align_bytes=64)
        gain = keep.tile([P, D], BF16, name="gain", align_bytes=64)
        raw_tiles = []

        def load_raw(i):
            t = raws.tile([P, 4, D], BF16, name="raw", tag="raw", align_bytes=64)
            view = raw_src[i // 4].rearrange("(g p t) n -> g p t n", p=P, t=4)
            nc.sync.dma_start(out=t[:], in_=view[i % 4])
            raw_tiles.append(t)

        wide_tiles = {}
        group_tiles = {}
        code_tiles = {}

        def widen(i):
            _, g, _, width, _ = chunks[i]
            t = pools["share"].tile([P, 4, 1024], BF16, name="wide", tag="wide", bufs=3, align_bytes=64)
            wide_tiles[i] = t
            src = byte_tiles[i]
            for j in range(4):
                col = scale[:, g, j : j + 1]
                cut = max(0, min(width, PARAMS["ws"][i] - j * width))
                if cut:
                    nc.scalar.activation(out=t[:, j, 0:cut], in_=src[:, j, 0:cut].bitcast(FP8), func=ACT.Copy, scale=col)
                if cut < width:
                    nc.vector.tensor_scalar(
                        out=t[:, j, cut:width], in0=src[:, j, cut:width].bitcast(FP8), scalar1=col, scalar2=None, op0=MULT
                    )

        def source(i):
            name, _, c0, width, raw = chunks[i]
            if name == "share":
                return wide_tiles[i][:, :, 0:width]
            return raw_tiles[raw][:, :, c0 : c0 + width]

        tensor_tiles = {}
        tensor_done = set()

        def tensor_interleave(i):
            width = chunks[i][3]
            pt = psum.tile([P, 1024], BF16, name="pt", tag="bank%d" % bank_of[i])
            for m in range(2):
                c = width - 256 + 128 * m
                nc.tensor.matmul(
                    pt[:, 512 * m : 512 * (m + 1)],
                    lhsT=ident_bf[:],
                    rhs=source(i)[:, :, c : c + 128].rearrange("p t n -> p n t"),
                    start=True,
                    stop=True,
                )
            tensor_tiles[i] = pt

        def interleave(i):
            width = chunks[i][3]
            src = source(i)
            dst = groups.tile([P, 4 * width], BF16, name="group", tag="group", align_bytes=64)
            group_tiles[i] = dst
            v_end = vector_cols(i)
            s_end = width - tensor_cols.get(i, 0)
            if s_end < width:
                nc.scalar.copy(out=dst[:, 4 * s_end : 4 * width], in_=tensor_tiles.pop(i)[:])
            for copy, lo, hi in ((nc.scalar.copy, v_end, s_end), (nc.vector.tensor_copy, 0, v_end)):
                if lo == hi:
                    continue
                copy(
                    out=dst[:, 4 * lo : 4 * hi].rearrange("p (c i t) -> p c t i", i=4, t=4),
                    in_=src[:, :, lo:hi].rearrange("p t (c i) -> p c t i", i=4),
                )

        def quantize(i):
            width = chunks[i][3]
            codes = quant.tile([P, width], U32, name="wq", tag="wq", align_bytes=64)
            scales = quant.tile([P, width], U8, name="ws", tag="ws", align_bytes=64)
            nc.vector.quantize_mx(out=codes[:].bitcast(FP8X4), scales=scales[:], in_=group_tiles.pop(i)[:])
            code_tiles[i] = (codes, scales)

        def bank(b, shape, name):
            return psum.tile(shape, F32, name=name, tag="bank%d" % b)

        def transpose_half(x, half, b):
            words = x[:].bitcast(F32)
            xt = bank(b, [P, 4, T], "xt")
            for gl in range(2):
                g = 2 * half + gl
                for u in range(2):
                    nc.tensor.transpose(xt[:, 2 * gl + u, :], words[:, 256 * g + u : 256 * (g + 1) : 2], ident[:])
            return xt

        def regroup_half(copy, dst, xt, half):
            copy(
                out=dst[:].bitcast(F32)[:, 512 * half : 512 * (half + 1)].rearrange("p (g r u) -> p g r u", g=2, u=2),
                in_=xt[:].rearrange("p (g u) r -> p g r u", g=2),
            )

        def new_operand(name):
            grouped = keep.tile([P, 4 * 4 * T], BF16, name="xgroup", tag="xgroup", bufs=1, align_bytes=64)
            codes = keep.tile([P, 4 * T], U32, name=name + "_q", align_bytes=64)
            scales = keep.tile([P, 4 * T], U8, name=name + "_s", align_bytes=64)
            return grouped, codes, scales

        def quantize_operand(x, lo, hi):
            grouped, codes, scales = x
            nc.vector.quantize_mx(
                out=codes[:, lo:hi].bitcast(FP8X4), scales=scales[:, lo:hi], in_=grouped[:, 4 * lo : 4 * hi]
            )

        acc = {}
        operand = {}

        delta_bank = {0: 0, 512: 1, 1024: 2, 1536: 3, 1792: 4, 1920: 5}

        def multiply(i):
            name, g, c0, width, _ = chunks[i]
            codes, scales = code_tiles.pop(i)
            _, xq, xs = operand[name]
            n = min(width, 512)
            for n0 in range(0, width, n):
                col = c0 + n0
                first = name in ("share", "gate", "delta") and g == 0
                last = name in ("recv", "gate", "delta") and g == 3
                key = ("u" if name in ("share", "recv") else name, col)
                if first:
                    b = delta_bank[col] if name == "delta" else col // 512 + (4 if name == "gate" else 0)
                    acc[key] = bank(b, [T, 512], "acc")
                nc.tensor.matmul_mx(
                    out=acc[key][:, 0:n],
                    lhsT=xq[:, g * T : (g + 1) * T].bitcast(FP8X4),
                    lhsT_scale=xs[:, g * T : (g + 1) * T],
                    rhs=codes[:, n0 : n0 + n].bitcast(FP8X4),
                    rhs_scale=scales[:, n0 : n0 + n],
                    start=first,
                    stop=last,
                )

        late = {}

        def silu(col):
            t = pools["late"].tile([T, 512], F32, name="act", tag="act", bufs=4)
            nc.scalar.activation(out=t[:], in_=acc[("u", col)][:], func=ACT.Silu)
            late["act", col] = t

        def gain_mul(col):
            cols = slice(col, col + 512)
            nc.vector.tensor_tensor(out=late["h"][:, cols], in0=late["act", col][:], in1=gain[:, cols], op=MULT)

        def half_tanh(col):
            nc.scalar.activation(out=late["gate"][:, col : col + 512], in_=acc[("gate", col)][:], func=ACT.Tanh, scale=0.5)

        def gated(col, width=512):
            t = pools["late"].tile([T, width], F32, name="prod", tag="prod", bufs=3)
            nc.vector.scalar_tensor_tensor(
                out=t[:],
                in0=late["gate"][:, col : col + width],
                scalar=1.0,
                in1=acc[("delta", col)][:, 0:width],
                op0=ADD,
                op1=MULT,
            )
            late["prod", col] = t

        def residual(col, width=512):
            cols = slice(col, col + width)
            t = pools["late"].tile([T, width], F32, name="res", tag="res", bufs=3)
            nc.vector.scalar_tensor_tensor(
                out=t[:], in0=late["prod", col][:], scalar=0.5, in1=kr[:, cols], op0=MULT, op1=ADD
            )
            nc.sync.dma_start(out=out[:, cols], in_=t[:])

        operand["share"] = new_operand("ks")
        operand["recv"] = new_operand("kr")
        xt = {}
        gate_next = [G]

        tail_calls = {}
        done = L
        for c0, width in PARAMS["tail"]:
            done += 4
            for k, col in enumerate(range(c0, c0 + width, 512)):
                args = (col, min(width, 512))
                last = (c0 + width) == D
                tail_calls.setdefault(10**6 if last else done + 1 + k, []).append((args, gated))
                tail_calls.setdefault(10**6 if last else done + 2 + k, []).append((args, residual))

        def step(s):
            i = s + 2
            if 0 <= i < n_chunks:
                interleave(i)
                name, g, c0, width, raw = chunks[i]
                if name in ("recv", "gate") and c0 == 1024 and raw + 5 < 12:
                    load_raw(raw + 5)
            if s + 4 < n_share:
                widen(s + 4)
            for i in (s + 5 if s + 5 < G else s + 4, s + 4):
                if i in tensor_cols and i not in tensor_done:
                    tensor_done.add(i)
                    tensor_interleave(i)

            if s == -1:
                xt[0] = transpose_half(early["ks"], 0, 4)
                xt[1] = transpose_half(early["ks"], 1, 5)
            if s == 0:
                regroup_half(nc.scalar.copy, operand["share"][0], xt[0], 0)
                regroup_half(nc.scalar.copy, operand["share"][0], xt[1], 1)
            if s == 2:
                quantize_operand(operand["share"], 0, 512)
            if s == 3:
                xt[0] = transpose_half(kr, 0, 6)
                xt[1] = transpose_half(kr, 1, 7)
            if s == 4:
                regroup_half(nc.scalar.copy, operand["recv"][0], xt[0], 0)
                regroup_half(nc.scalar.copy, operand["recv"][0], xt[1], 1)
            if s == 7:
                quantize_operand(operand["recv"], 0, 512)
            if s == G - 1:
                silu(0)
                silu(512)
            if s == G:
                silu(1024)
                silu(1536)
                gain_mul(0)
                gain_mul(512)
                operand["gate"] = operand["delta"] = new_operand("hq")
                xt[0] = transpose_half(late["h"], 0, 6)
            if s == G + 1:
                regroup_half(nc.scalar.copy, operand["gate"][0], xt[0], 0)
                gain_mul(1024)
                gain_mul(1536)
                xt[1] = transpose_half(late["h"], 1, 7)
            if s == G + 2:
                quantize_operand(operand["gate"], 0, 256)
                regroup_half(nc.scalar.copy, operand["gate"][0], xt[1], 1)
            if s == G + 3:
                quantize_operand(operand["gate"], 256, 512)
            if s == L:
                half_tanh(0)
                half_tanh(512)
            if s == L + 1:
                half_tanh(1024)
                half_tanh(1536)
            for when, call in tail_calls.get(s, []):
                call(*when)

            if s >= 0:
                quantize(s)
                if s == 2:
                    multiply(0)
                    multiply(1)
                if 2 <= s < G:
                    multiply(s)
                elif s >= G + 2:
                    stop = min(gate_next[0] + 2, s + 1)
                    for k in range(gate_next[0], stop):
                        multiply(k)
                    gate_next[0] = stop

        with tc.tile_pool(name="share", bufs=1) as share:
            pools["share"] = share
            early["ks"] = share.tile([T, D], BF16, name="ks", align_bytes=64)
            for i in range(3):
                load_bytes(i)
            nc.sync.dma_start(out=early["ks"][:], in_=k_share)
            for i in range(3, n_share):
                load_bytes(i)
            nc.sync.dma_start(out=kr[:], in_=k_recv)
            load_raw(0)
            load_raw(1)
            nc.sync.dma_start(out=gain[:], in_=g_hid.partition_broadcast(P))
            for i in range(2, 5):
                load_raw(i)
            for s in range(-4, n_share):
                step(s)

        with tc.tile_pool(name="late", bufs=1) as late_pool:
            pools["late"] = late_pool
            late["h"] = late_pool.tile([T, D], BF16, name="h", align_bytes=64)
            late["gate"] = late_pool.tile([T, D], F32, name="gate")
            for s in range(n_share, n_chunks):
                step(s)
            for when, call in tail_calls[10**6]:
                call(*when)
